import numpy as np
import ml_dtypes


def mxq(x, axis, fmt="e4m3"):
    dtype, down = {"e4m3": (ml_dtypes.float8_e4m3fn, 7), "e5m2": (ml_dtypes.float8_e5m2, 14)}[fmt]
    v = np.moveaxis(np.asarray(x, np.float32).astype(ml_dtypes.bfloat16).astype(np.float64), axis, -1)
    blocks = v.reshape(v.shape[:-1] + (-1, 32))
    amax = np.abs(blocks).max(-1, keepdims=True)
    byte = np.maximum(np.where(amax > 0, np.frexp(amax)[1] - 1 + 127, 0) - down, 1)
    scale = np.exp2(byte - 127.0)
    codes = (blocks / scale).astype(np.float32).astype(dtype).astype(np.float64)
    return np.moveaxis((codes * scale).reshape(v.shape), -1, axis)


WIDE = False


def mx_kscale(k):
    if not WIDE:
        return np.ones(k)
    levels = np.array([10, -10, 5, -5, 0])
    if k % 512:
        return np.exp2(np.random.permutation(np.resize(levels, k // 32))).repeat(32)
    a = np.empty((k // 512, 16))
    for p in range(k // 512):
        a[p, :8] = np.random.permutation(np.resize(levels, 8))
        for g in range(8):
            far = levels[np.abs(levels - a[p, g]) >= 10]
            a[p, g + 8] = far[np.random.randint(len(far))]
    return np.exp2(a.ravel()).repeat(32)


def f64(x):
    return np.asarray(x).astype(np.float64)


def striped(idx):
    return np.tile(idx.reshape(-1, 16).T, (8, 1)).astype(np.uint16)


def unstriped(offs):
    return offs[:16].T.reshape(-1).astype(np.int64)


def striped8(idx):
    return np.concatenate([x.reshape(-1, 16).T for x in idx]).astype(np.uint16)


def runs(offs, k):
    lists = np.stack([offs[16 * r : 16 * r + 16].T.reshape(-1) for r in range(8)]).astype(np.int64)
    return lists[np.arange(k) % 512 // 64]


def pack_weight(w):
    k, n = w.shape
    w = f64(np.asarray(w, np.float32).astype(ml_dtypes.bfloat16)).reshape(k // 32, 32, n)
    amax = np.abs(w).max(1)
    byte = np.clip(np.where(amax > 0, np.frexp(amax)[1] - 1 + 127 - 7, 1), 1, 254)
    scaled = (w * np.exp2(127.0 - byte)[:, None, :]).reshape(k, n).astype(np.float32)
    words = np.ascontiguousarray(scaled.reshape(k // 512, 128, 4, n).transpose(0, 1, 3, 2)).astype(ml_dtypes.float8_e4m3fn).view(np.uint8)
    return words, np.ascontiguousarray(byte.astype(np.uint8).reshape(k // 512, 16, n))


def unpack_weight(words, scales):
    g, p, n, _ = words.shape
    vals = np.ascontiguousarray(words).view(ml_dtypes.float8_e4m3fn).astype(np.float64) * np.repeat(np.exp2(scales.astype(np.float64) - 127.0), 8, axis=1)[..., None]
    return vals.transpose(0, 1, 3, 2).reshape(g * 512, n)


K, T, S, N, H, W = 512, 2048, 512, 512, 512, 256


def setup_inputs():
    n = np.random.standard_normal
    s = mx_kscale(K)[:, None]
    u = mx_kscale(H)
    packed_xT = pack_weight(n((K, T)) * s)
    return {
        "x_words": packed_xT[0],
        "x_scales": packed_xT[1],
        "w1": (n((K, H)) / np.sqrt(K) / s).astype(np.float32),
        "w2": (n((K, H)) / np.sqrt(K) / s).astype(np.float32),
        "w3": (n((K, H)) / np.sqrt(K) / s).astype(np.float32),
        "gn": (np.random.uniform(0.5, 1.5, (H, 1)) * u[:, None]).astype(np.float32),
        "w4": (n((H, N)) / np.sqrt(H) / u[:, None]).astype(np.float32),
        "offs": striped(np.random.permutation(T)[:S]),
        "two": striped(np.random.permutation(T)[:S]),
        "three": striped(np.random.permutation(T)[:S]),
        "n1": striped8(np.stack([np.random.permutation(S)[:W] for _ in range(8)])),
        "n2": striped8(np.stack([np.random.permutation(S)[:W] for _ in range(8)])),
        "n3": striped8(np.stack([np.random.permutation(S) for _ in range(8)])),
        "n4": striped8(np.stack([np.random.permutation(S) for _ in range(8)])),
        "n5": striped8(np.stack([np.random.permutation(S) for _ in range(8)])),
        "n6": striped8(np.stack([np.random.permutation(S) for _ in range(8)])),
        "n7": striped8(np.stack([np.random.permutation(S) for _ in range(8)])),
    }


def reference(x_words, x_scales, w1, w2, w3, gn, w4, offs, two, three, n1, n2, n3, n4, n5, n6, n7):
    x_two = unpack_weight(x_words, x_scales)[:, unstriped(two)]
    d = mxq(f64(w2), 0, "e4m3").T @ x_two
    xq = unpack_weight(x_words, x_scales)[:, unstriped(offs)]
    y = mxq(f64(w1), 0, "e4m3").T @ xq
    ra = d[np.arange(H)[:, None], runs(n2, H)] - (0.5 * (y[np.arange(H)[:, None], runs(n1, H)]))
    m1 = y.copy()
    m1[np.arange(H)[:, None], runs(n1, H)] = ra
    x_three = unpack_weight(x_words, x_scales)[:, unstriped(three)]
    b = mxq(f64(w3), 0, "e4m3").T @ x_three
    z = f64(gn) * (np.maximum(m1[np.arange(H)[:, None], runs(n3, H)] + b[np.arange(H)[:, None], runs(n5, H)], m1[np.arange(H)[:, None], runs(n4, H)] + b[np.arange(H)[:, None], runs(n6, H)]))
    h = mxq(f64(w4), 0, "e4m3").T @ mxq(z, 0, "e4m3")
    pa = h[np.arange(N)[:, None], runs(n7, N)]
    return (2.0 * (h * pa)) / ((h) ** 2 + (pa) ** 2 + 0.5)

@@ -1,0 +1,207 @@
+from contextlib import ExitStack
+
+import concourse.mybir as mybir
+
+K, T, S, N, H, W = 512, 2048, 512, 512, 512, 256
+FLOPS = 4 * 2 * 512 * 512 * 512
+
+F32 = mybir.dt.float32
+BF16 = mybir.dt.bfloat16
+I32 = mybir.dt.int32
+U32 = mybir.dt.uint32
+U16 = mybir.dt.uint16
+U8 = mybir.dt.uint8
+FP8X4 = mybir.dt.float8_e4m3fn_x4
+ALU = mybir.AluOpType
+ACT = mybir.ActivationFunctionType
+
+P = 128
+PACK = 4
+STRIPE = 16
+PIECE = 256
+
+
+def tile_picked_trioputbpathbharm_none_p_kernel(
+    tc, x_words, x_scales, w1, w2, w3, gn, w4, offs, two, three, n1, n2, n3, n4, n5, n6, n7, out
+):
+    nc = tc.nc
+    with ExitStack() as ctx:
+        keep = ctx.enter_context(tc.tile_pool(name="keep", bufs=1))
+        ring = ctx.enter_context(tc.tile_pool(name="ring", bufs=3))
+        psum = ctx.enter_context(tc.psum_pool(name="psum", bufs=1))
+
+        def load_list(name, src):
+            tile = keep.tile(list(src.shape), U16, name=name)
+            nc.sync.dma_start(tile[:], src)
+            return tile
+
+        def load_weight(name, src, parts):
+            width = H // parts
+            view = src.rearrange("(p j) c -> p j c", j=PACK)
+            raws = []
+            for part in range(parts):
+                raw = keep.tile([P, PACK, width], F32, name=f"{name}_raw{part}")
+                nc.sync.dma_start(raw[:], view[:, :, part * width : (part + 1) * width])
+                raws.append(raw)
+            return raws
+
+        def cast_weight(name, raws):
+            grouped = keep.tile([P, PACK * H], BF16, name=f"{name}_bf16", align_bytes=64)
+            dealt = grouped[:].rearrange("p (t m j) -> p m j t", t=PACK, j=PACK)
+            rows = P // len(raws)
+            for part, raw in enumerate(raws):
+                nc.scalar.copy(dealt[:, part * rows : (part + 1) * rows], raw[:].rearrange("p j (m t) -> p m j t", t=PACK))
+            return grouped
+
+        def quantize(name, grouped):
+            width = grouped.shape[1] // PACK
+            codes = keep.tile([P, width], U32, name=f"{name}_codes", align_bytes=64)
+            scales = keep.tile([P, width], U8, name=f"{name}_scales", align_bytes=64)
+            nc.vector.quantize_mx(out=codes[:].bitcast(FP8X4), scales=scales[:], in_=grouped[:])
+            return codes, scales
+
+        def product(bank, weight, t, moving):
+            cols = slice(t * P, (t + 1) * P)
+            nc.tensor.matmul_mx(
+                out=bank,
+                lhsT=weight[0][:, cols].bitcast(FP8X4),
+                lhsT_scale=weight[1][:, cols],
+                rhs=moving[0][:].bitcast(FP8X4),
+                rhs_scale=moving[1][:],
+                start=True,
+                stop=True,
+            )
+
+        scale_table = keep.tile([P, T], U8, name="scale_table", align_bytes=64)
+        nc.gpsimd.memset(scale_table[:].bitcast(I32), 0)
+        l_offs = load_list("l_offs", offs)
+        warm = keep.tile([P, 2], F32, name="warm")
+        nc.vector.memset(warm[:, 0:1], 1.0)
+        nc.scalar.activation(warm[:, 1:2], warm[:, 0:1], ACT.Abs_reciprocal_sqrt)
+
+        l_two = load_list("l_two", two)
+        l_three = load_list("l_three", three)
+        for q in range(4):
+            nc.sync.dma_start(scale_table[32 * q : 32 * q + 4, :].bitcast(I32), x_scales[0, 4 * q : 4 * q + 4, :].bitcast(I32))
+        w1_raw = load_weight("w1", w1, 1)
+        word_table = keep.tile([P, T], I32, name="word_table", align_bytes=64)
+        nc.sync.dma_start(word_table[:], x_words[0].rearrange("p n t -> p (n t)").bitcast(I32))
+        w2_raw = load_weight("w2", w2, 2)
+        l_n1 = load_list("l_n1", n1)
+        l_n2 = load_list("l_n2", n2)
+        w3_raw = load_weight("w3", w3, 1)
+        l_n3 = load_list("l_n3", n3)
+        l_n5 = load_list("l_n5", n5)
+        l_n4 = load_list("l_n4", n4)
+        l_n6 = load_list("l_n6", n6)
+        gain = keep.tile([P, PACK], F32, name="gain")
+        nc.sync.dma_start(gain[:], gn.rearrange("(p t) o -> p (t o)", t=PACK))
+        w4_raw = load_weight("w4", w4, 1)
+        l_n7 = load_list("l_n7", n7)
+
+        def pick_scales(name, lst):
+            picked = keep.tile([P, S], U8, name=f"{name}_scales", align_bytes=64)
+            nc.vector.tensor_copy(picked[:], scale_table[:].indirect(lst[:]))
+            return picked
+
+        def pick_words(name, lst):
+            picked = keep.tile([P, S], U32, name=f"{name}_words", align_bytes=64)
+            nc.vector.tensor_copy(picked[:], word_table[:].bitcast(U32).indirect(lst[:]))
+            return picked
+
+        def bank(number):
+            return psum.tile([P, S], F32, name=f"bank{number}")
+
+        def leave_bank(name, src):
+            tile = keep.tile([P, S], F32, name=name)
+            nc.scalar.copy(tile[:], src[:])
+            return tile
+
+        s_offs = pick_scales("x_offs", l_offs)
+        s_two = pick_scales("x_two", l_two)
+        s_three = pick_scales("x_three", l_three)
+        w1_bf16 = cast_weight("w1", w1_raw)
+        x_offs = (pick_words("x_offs", l_offs), s_offs)
+        w1_q = quantize("w1", w1_bf16)
+        x_two = (pick_words("x_two", l_two), s_two)
+        w2_bf16 = cast_weight("w2", w2_raw)
+        y_banks = [bank(t) for t in range(PACK)]
+        for t in range(PACK):
+            product(y_banks[t][:], w1_q, t, x_offs)
+        x_three = (pick_words("x_three", l_three), s_three)
+        w2_q = quantize("w2", w2_bf16)
+        d_banks = [bank(PACK + t) for t in range(PACK)]
+        for t in range(PACK):
+            product(d_banks[t][:], w2_q, t, x_two)
+
+        m1, d = [], []
+        for t in range(PACK):
+            m1.append(leave_bank(f"m1_{t}", y_banks[t]))
+            d.append(leave_bank(f"d_{t}", d_banks[t]))
+        w3_bf16 = cast_weight("w3", w3_raw)
+
+        for t in range(PACK):
+            half_y = ring.tile([P, W], F32, name="half_y")
+            picked_d = ring.tile([P, W], F32, name="picked_d")
+            nc.vector.tensor_scalar(half_y[:], m1[t][:].indirect(l_n1[:]), -0.5, 0.0, ALU.mult, ALU.add)
+            nc.vector.tensor_copy(picked_d[:], d[t][:].indirect(l_n2[:]))
+            if t == PACK - 2:
+                w3_q = quantize("w3", w3_bf16)
+            nc.vector.tensor_tensor(m1[t][:].indirect(l_n1[:]), half_y[:], picked_d[:], ALU.add)
+
+        b = []
+        for t in range(PACK):
+            b_bank = bank(t)
+            product(b_bank[:], w3_q, t, x_three)
+            b.append(leave_bank(f"b_{t}", b_bank))
+        w4_bf16 = cast_weight("w4", w4_raw)
+
+        h_banks = [bank(PACK + t) for t in range(PACK)]
+        h_pairs = [keep.tile([P, 2 * S], F32, name=f"h_pair{t}") for t in range(PACK)]
+        h_squares = [keep.tile([P, S], F32, name=f"h_square{t}") for t in range(PACK)]
+        for piece in range(S // PIECE):
+            entries = slice(piece * PIECE // STRIPE, (piece + 1) * PIECE // STRIPE)
+            cols = slice(piece * PIECE, (piece + 1) * PIECE)
+            z_bf16 = keep.tile([P, PACK * PIECE], BF16, name=f"z_bf16_{piece}", align_bytes=64)
+            z_planes = z_bf16[:].rearrange("p (j t) -> p j t", t=PACK)
+            for t in range(PACK):
+                first_m = ring.tile([P, PIECE], F32, name="first_m")
+                second_m = ring.tile([P, PIECE], F32, name="second_m")
+                first = ring.tile([P, PIECE], F32, name="first")
+                second = ring.tile([P, PIECE], F32, name="second")
+                larger = h_pairs[t][:, S + piece * PIECE : S + (piece + 1) * PIECE]
+                nc.vector.tensor_copy(first_m[:], m1[t][:].indirect(l_n3[:, entries]))
+                nc.vector.tensor_copy(second_m[:], m1[t][:].indirect(l_n4[:, entries]))
+                nc.vector.tensor_tensor(first[:], b[t][:].indirect(l_n5[:, entries]), first_m[:], ALU.add)
+                nc.vector.tensor_tensor(second[:], b[t][:].indirect(l_n6[:, entries]), second_m[:], ALU.add)
+                nc.vector.tensor_tensor(larger, first[:], second[:], ALU.max)
+                nc.scalar.activation(z_planes[:, :, t], larger, ACT.Copy, scale=gain[:, t : t + 1])
+            if piece == 0:
+                w4_q = quantize("w4", w4_bf16)
+            z_q = quantize(f"z{piece}", z_bf16)
+            for t in range(PACK):
+                product(h_banks[t][:, cols], w4_q, t, z_q)
+            for t in range(PACK):
+                nc.scalar.copy(h_pairs[t][:, cols], h_banks[t][:, cols])
+            for t in range(PACK):
+                nc.scalar.activation(h_squares[t][:, cols], h_banks[t][:, cols], ACT.Square)
+
+        out_rows = out.rearrange("(p t) j -> p t j", t=PACK)
+        partner = [keep.tile([P, S], F32, name=f"partner{t}") for t in range(PACK)]
+        top = [keep.tile([P, S], F32, name=f"top{t}") for t in range(PACK)]
+        inverse = [keep.tile([P, S], F32, name=f"inverse{t}") for t in range(PACK)]
+        squares = [keep.tile([P, S], F32, name=f"square{t}") for t in range(PACK)]
+        sums = [keep.tile([P, S], F32, name=f"sum{t}") for t in range(PACK)]
+        for t in range(PACK):
+            nc.vector.tensor_copy(partner[t][:], h_pairs[t][:].indirect(l_n7[:]))
+            nc.scalar.activation(squares[t][:], partner[t][:], ACT.Square)
+            nc.vector.tensor_tensor(sums[t][:], squares[t][:], h_squares[t][:], ALU.add)
+        for t in range(PACK):
+            root = ring.tile([P, S], F32, name="root")
+            nc.vector.scalar_tensor_tensor(top[t][:], h_banks[t][:], 2.0, partner[t][:], ALU.mult, ALU.mult)
+            nc.scalar.activation(root[:], sums[t][:], ACT.Abs_reciprocal_sqrt, bias=0.5)
+            nc.scalar.activation(inverse[t][:], root[:], ACT.Square)
+        for t in range(PACK):
+            result = ring.tile([P, S], F32, name="result")
+            nc.vector.tensor_tensor(result[:], top[t][:], inverse[t][:], ALU.mult)
+            nc.sync.dma_start(out_rows[:, t, :], result[:])

@@ -1,6 +1,7 @@
 from contextlib import ExitStack
 
 import concourse.mybir as mybir
+from concourse.masks import make_identity
 
 K, T, S, N, H, W = 512, 2048, 512, 512, 512, 256
 FLOPS = 4 * 2 * 512 * 512 * 512
@@ -47,10 +48,10 @@ def tile_picked_trioputbpathbharm_none_p_kernel(
 
         def cast_weight(name, raws):
             grouped = keep.tile([P, PACK * H], BF16, name=f"{name}_bf16", align_bytes=64)
-            dealt = grouped[:].rearrange("p (t m j) -> p m j t", t=PACK, j=PACK)
-            rows = P // len(raws)
+            dealt = grouped[:].rearrange("p (t u i j) -> p t u j i", t=PACK, i=PACK, j=PACK)
+            groups = P // PACK // len(raws)
             for part, raw in enumerate(raws):
-                nc.scalar.copy(dealt[:, part * rows : (part + 1) * rows], raw[:].rearrange("p j (m t) -> p m j t", t=PACK))
+                nc.scalar.copy(dealt[:, :, part * groups : (part + 1) * groups], raw[:].rearrange("p j (u t i) -> p t u j i", t=PACK, i=PACK))
             return grouped
 
         def quantize(name, grouped):
@@ -74,6 +75,8 @@ def tile_picked_trioputbpathbharm_none_p_kernel(
 
         scale_table = keep.tile([P, T], U8, name="scale_table", align_bytes=64)
         nc.gpsimd.memset(scale_table[:].bitcast(I32), 0)
+        identity = keep.tile([P, P], F32, name="identity")
+        make_identity(nc, identity[:])
         l_offs = load_list("l_offs", offs)
         warm = keep.tile([P, 2], F32, name="warm")
         nc.vector.memset(warm[:, 0:1], 1.0)
@@ -94,9 +97,13 @@ def tile_picked_trioputbpathbharm_none_p_kernel(
         l_n5 = load_list("l_n5", n5)
         l_n4 = load_list("l_n4", n4)
         l_n6 = load_list("l_n6", n6)
-        gain = keep.tile([P, PACK], F32, name="gain")
-        nc.sync.dma_start(gain[:], gn.rearrange("(p t) o -> p (t o)", t=PACK))
-        w4_raw = load_weight("w4", w4, 1)
+        gain = [keep.tile([P, 1], F32, name=f"gain{t}") for t in range(PACK)]
+        for t in range(PACK):
+            nc.sync.dma_start(gain[t][:], gn.rearrange("(u t i) o -> t u i o", t=PACK, i=PACK)[t])
+        w4_tile = keep.tile([P, PACK, N], F32, name="w4_raw")
+        for t in range(PACK):
+            nc.sync.dma_start(w4_tile[:, t, :], w4.rearrange("(u t i) c -> t u i c", t=PACK, i=PACK)[t])
+        w4_raw = [w4_tile]
         l_n7 = load_list("l_n7", n7)
 
         def pick_scales(name, lst):
@@ -140,14 +147,14 @@ def tile_picked_trioputbpathbharm_none_p_kernel(
             d.append(leave_bank(f"d_{t}", d_banks[t]))
         w3_bf16 = cast_weight("w3", w3_raw)
 
+        half_y = [keep.tile([P, W], F32, name=f"half_y{t}") for t in range(PACK)]
+        picked_d = [keep.tile([P, W], F32, name=f"picked_d{t}") for t in range(PACK)]
         for t in range(PACK):
-            half_y = ring.tile([P, W], F32, name="half_y")
-            picked_d = ring.tile([P, W], F32, name="picked_d")
-            nc.vector.tensor_scalar(half_y[:], m1[t][:].indirect(l_n1[:]), -0.5, 0.0, ALU.mult, ALU.add)
-            nc.vector.tensor_copy(picked_d[:], d[t][:].indirect(l_n2[:]))
-            if t == PACK - 2:
-                w3_q = quantize("w3", w3_bf16)
-            nc.vector.tensor_tensor(m1[t][:].indirect(l_n1[:]), half_y[:], picked_d[:], ALU.add)
+            nc.vector.tensor_scalar(half_y[t][:], m1[t][:].indirect(l_n1[:]), -0.5, 0.0, ALU.mult, ALU.add)
+            nc.vector.tensor_copy(picked_d[t][:], d[t][:].indirect(l_n2[:]))
+        w3_q = quantize("w3", w3_bf16)
+        for t in range(PACK):
+            nc.vector.tensor_tensor(m1[t][:].indirect(l_n1[:]), half_y[t][:], picked_d[t][:], ALU.add)
 
         b = []
         for t in range(PACK):
@@ -159,26 +166,34 @@ def tile_picked_trioputbpathbharm_none_p_kernel(
         h_banks = [bank(PACK + t) for t in range(PACK)]
         h_pairs = [keep.tile([P, 2 * S], F32, name=f"h_pair{t}") for t in range(PACK)]
         h_squares = [keep.tile([P, S], F32, name=f"h_square{t}") for t in range(PACK)]
-        for piece in range(S // PIECE):
+        z_bf16 = [keep.tile([P, PACK * PIECE], BF16, name=f"z_bf16_{piece}", align_bytes=64) for piece in range(S // PIECE)]
+        w4_q = quantize("w4", w4_bf16)
+
+        def fetch_m1(piece, t):
             entries = slice(piece * PIECE // STRIPE, (piece + 1) * PIECE // STRIPE)
+            first_m = ring.tile([P, PIECE], F32, name="first_m")
+            second_m = ring.tile([P, PIECE], F32, name="second_m")
+            nc.vector.tensor_copy(first_m[:], m1[t][:].indirect(l_n3[:, entries]))
+            nc.vector.tensor_copy(second_m[:], m1[t][:].indirect(l_n4[:, entries]))
+            return first_m, second_m
+
+        def add_b(piece, t, first_m, second_m):
+            entries = slice(piece * PIECE // STRIPE, (piece + 1) * PIECE // STRIPE)
+            first = ring.tile([P, PIECE], F32, name="first")
+            second = ring.tile([P, PIECE], F32, name="second")
+            nc.vector.tensor_tensor(first[:], b[t][:].indirect(l_n5[:, entries]), first_m[:], ALU.add)
+            nc.vector.tensor_tensor(second[:], b[t][:].indirect(l_n6[:, entries]), second_m[:], ALU.add)
+            return first, second
+
+        def make_z(piece, t, first, second):
+            larger = h_pairs[t][:, S + piece * PIECE : S + (piece + 1) * PIECE]
+            nc.vector.tensor_tensor(larger, first[:], second[:], ALU.max)
+            z_planes = z_bf16[piece][:].rearrange("p (j t) -> p j t", t=PACK)
+            nc.scalar.activation(z_planes[:, :, t], larger, ACT.Copy, scale=gain[t][:])
+
+        def make_h(piece):
             cols = slice(piece * PIECE, (piece + 1) * PIECE)
-            z_bf16 = keep.tile([P, PACK * PIECE], BF16, name=f"z_bf16_{piece}", align_bytes=64)
-            z_planes = z_bf16[:].rearrange("p (j t) -> p j t", t=PACK)
-            for t in range(PACK):
-                first_m = ring.tile([P, PIECE], F32, name="first_m")
-                second_m = ring.tile([P, PIECE], F32, name="second_m")
-                first = ring.tile([P, PIECE], F32, name="first")
-                second = ring.tile([P, PIECE], F32, name="second")
-                larger = h_pairs[t][:, S + piece * PIECE : S + (piece + 1) * PIECE]
-                nc.vector.tensor_copy(first_m[:], m1[t][:].indirect(l_n3[:, entries]))
-                nc.vector.tensor_copy(second_m[:], m1[t][:].indirect(l_n4[:, entries]))
-                nc.vector.tensor_tensor(first[:], b[t][:].indirect(l_n5[:, entries]), first_m[:], ALU.add)
-                nc.vector.tensor_tensor(second[:], b[t][:].indirect(l_n6[:, entries]), second_m[:], ALU.add)
-                nc.vector.tensor_tensor(larger, first[:], second[:], ALU.max)
-                nc.scalar.activation(z_planes[:, :, t], larger, ACT.Copy, scale=gain[:, t : t + 1])
-            if piece == 0:
-                w4_q = quantize("w4", w4_bf16)
-            z_q = quantize(f"z{piece}", z_bf16)
+            z_q = quantize(f"z{piece}", z_bf16[piece])
             for t in range(PACK):
                 product(h_banks[t][:, cols], w4_q, t, z_q)
             for t in range(PACK):
@@ -186,22 +201,44 @@ def tile_picked_trioputbpathbharm_none_p_kernel(
             for t in range(PACK):
                 nc.scalar.activation(h_squares[t][:, cols], h_banks[t][:, cols], ACT.Square)
 
-        out_rows = out.rearrange("(p t) j -> p t j", t=PACK)
+        steps = [(piece, t) for piece in range(S // PIECE) for t in range(PACK)]
+        pending = None
+        for number, step in enumerate(steps):
+            fetched = fetch_m1(*step)
+            if pending is not None:
+                make_z(*steps[number - 1], *pending)
+            pending = add_b(*step, *fetched)
+            if step == (1, 0):
+                make_h(0)
+        make_z(*steps[-1], *pending)
+        make_h(1)
+
+        out_rows = out.rearrange("(u t i) j -> t u i j", t=PACK, i=PACK)
         partner = [keep.tile([P, S], F32, name=f"partner{t}") for t in range(PACK)]
         top = [keep.tile([P, S], F32, name=f"top{t}") for t in range(PACK)]
-        inverse = [keep.tile([P, S], F32, name=f"inverse{t}") for t in range(PACK)]
         squares = [keep.tile([P, S], F32, name=f"square{t}") for t in range(PACK)]
-        sums = [keep.tile([P, S], F32, name=f"sum{t}") for t in range(PACK)]
+        blocks = [slice(c, c + P) for c in range(0, S, P)]
+        turned = []
         for t in range(PACK):
             nc.vector.tensor_copy(partner[t][:], h_pairs[t][:].indirect(l_n7[:]))
             nc.scalar.activation(squares[t][:], partner[t][:], ACT.Square)
-            nc.vector.tensor_tensor(sums[t][:], squares[t][:], h_squares[t][:], ALU.add)
+            both = bank(t)
+            for block in blocks:
+                nc.tensor.matmul(both[:, block], h_squares[t][:, block], identity[:], start=True, stop=False, is_transpose=True)
+                nc.tensor.matmul(both[:, block], squares[t][:, block], identity[:], start=False, stop=True, is_transpose=True)
+            turned.append(both)
+        inverse = []
         for t in range(PACK):
             root = ring.tile([P, S], F32, name="root")
+            inverse_turned = ring.tile([P, S], F32, name="inverse_turned")
             nc.vector.scalar_tensor_tensor(top[t][:], h_banks[t][:], 2.0, partner[t][:], ALU.mult, ALU.mult)
-            nc.scalar.activation(root[:], sums[t][:], ACT.Abs_reciprocal_sqrt, bias=0.5)
-            nc.scalar.activation(inverse[t][:], root[:], ACT.Square)
+            nc.scalar.activation(root[:], turned[t][:], ACT.Abs_reciprocal_sqrt, bias=0.5)
+            nc.scalar.activation(inverse_turned[:], root[:], ACT.Square)
+            back = bank(t)
+            for block in blocks:
+                nc.tensor.transpose(back[:, block], inverse_turned[:, block], identity[:])
+            inverse.append(back)
         for t in range(PACK):
             result = ring.tile([P, S], F32, name="result")
-            nc.vector.tensor_tensor(result[:], top[t][:], inverse[t][:], ALU.mult)
-            nc.sync.dma_start(out_rows[:, t, :], result[:])
+            nc.vector.tensor_tensor(result[:], inverse[t][:], top[t][:], ALU.mult)
+            nc.sync.dma_start(out_rows[t], result[:])

@@ -74,21 +74,21 @@ def tile_picked_trioputbpathbharm_none_p_kernel(
             )
 
         scale_table = keep.tile([P, T], U8, name="scale_table", align_bytes=64)
-        nc.gpsimd.memset(scale_table[:].bitcast(I32), 0)
         identity = keep.tile([P, P], F32, name="identity")
         make_identity(nc, identity[:])
         l_offs = load_list("l_offs", offs)
+        for q in range(4):
+            rows = x_scales[0, 4 * q : 4 * q + 4, :].bitcast(I32)
+            nc.sync.dma_start(scale_table[32 * q : 32 * q + 32, :].bitcast(I32), rows.unsqueeze(0).broadcast_to([8, 4, T // 4]))
         warm = keep.tile([P, 2], F32, name="warm")
         nc.vector.memset(warm[:, 0:1], 1.0)
         nc.scalar.activation(warm[:, 1:2], warm[:, 0:1], ACT.Abs_reciprocal_sqrt)
 
         l_two = load_list("l_two", two)
-        l_three = load_list("l_three", three)
-        for q in range(4):
-            nc.sync.dma_start(scale_table[32 * q : 32 * q + 4, :].bitcast(I32), x_scales[0, 4 * q : 4 * q + 4, :].bitcast(I32))
-        w1_raw = load_weight("w1", w1, 1)
         word_table = keep.tile([P, T], I32, name="word_table", align_bytes=64)
         nc.sync.dma_start(word_table[:], x_words[0].rearrange("p n t -> p (n t)").bitcast(I32))
+        l_three = load_list("l_three", three)
+        w1_raw = load_weight("w1", w1, 2)
         w2_raw = load_weight("w2", w2, 2)
         l_n1 = load_list("l_n1", n1)
         l_n2 = load_list("l_n2", n2)
@@ -112,55 +112,55 @@ def tile_picked_trioputbpathbharm_none_p_kernel(
             return picked
 
         def pick_words(name, lst):
-            picked = keep.tile([P, S], U32, name=f"{name}_words", align_bytes=64)
+            picked = keep.tile([P, S], U32, name=name, align_bytes=64)
             nc.vector.tensor_copy(picked[:], word_table[:].bitcast(U32).indirect(lst[:]))
             return picked
 
         def bank(number):
             return psum.tile([P, S], F32, name=f"bank{number}")
 
-        def leave_bank(name, src):
-            tile = keep.tile([P, S], F32, name=name)
-            nc.scalar.copy(tile[:], src[:])
-            return tile
+        LAST = PACK - 1
+        m1 = [keep.tile([P, S if t == LAST else 2 * S], F32, name=f"m1_{t}") for t in range(PACK)]
+        b = [keep.tile([P, 2 * S], F32, name=f"b_{t}") for t in range(PACK)]
+        d = [keep.tile([P, S], F32, name=f"d_{t}") for t in range(PACK)]
+        for t in range(LAST):
+            nc.gpsimd.memset(m1[t][:, S:], 0.0)
 
         s_offs = pick_scales("x_offs", l_offs)
         s_two = pick_scales("x_two", l_two)
-        s_three = pick_scales("x_three", l_three)
         w1_bf16 = cast_weight("w1", w1_raw)
-        x_offs = (pick_words("x_offs", l_offs), s_offs)
+        x_offs = (pick_words("x_offs_words", l_offs), s_offs)
+        x_two = (pick_words("x_two_words", l_two), s_two)
+        s_three = pick_scales("x_three", l_three)
         w1_q = quantize("w1", w1_bf16)
-        x_two = (pick_words("x_two", l_two), s_two)
         w2_bf16 = cast_weight("w2", w2_raw)
         y_banks = [bank(t) for t in range(PACK)]
         for t in range(PACK):
             product(y_banks[t][:], w1_q, t, x_offs)
-        x_three = (pick_words("x_three", l_three), s_three)
+        x_three = (pick_words("w1_bf16", l_three), s_three)
         w2_q = quantize("w2", w2_bf16)
         d_banks = [bank(PACK + t) for t in range(PACK)]
         for t in range(PACK):
             product(d_banks[t][:], w2_q, t, x_two)
 
-        m1, d = [], []
         for t in range(PACK):
-            m1.append(leave_bank(f"m1_{t}", y_banks[t]))
-            d.append(leave_bank(f"d_{t}", d_banks[t]))
+            nc.scalar.copy(m1[t][:, :S], y_banks[t][:])
+            nc.scalar.copy(d[t][:], d_banks[t][:])
         w3_bf16 = cast_weight("w3", w3_raw)
 
-        half_y = [keep.tile([P, W], F32, name=f"half_y{t}") for t in range(PACK)]
-        picked_d = [keep.tile([P, W], F32, name=f"picked_d{t}") for t in range(PACK)]
+        half_y = [b[t][:, S : S + W] for t in range(PACK)]
+        picked_d = [b[t][:, S + W :] for t in range(PACK)]
         for t in range(PACK):
-            nc.vector.tensor_scalar(half_y[t][:], m1[t][:].indirect(l_n1[:]), -0.5, 0.0, ALU.mult, ALU.add)
-            nc.vector.tensor_copy(picked_d[t][:], d[t][:].indirect(l_n2[:]))
+            nc.vector.tensor_scalar(half_y[t], m1[t][:].indirect(l_n1[:]), -0.5, 0.0, ALU.mult, ALU.add)
+            nc.vector.tensor_copy(picked_d[t], d[t][:].indirect(l_n2[:]))
         w3_q = quantize("w3", w3_bf16)
         for t in range(PACK):
-            nc.vector.tensor_tensor(m1[t][:].indirect(l_n1[:]), half_y[t][:], picked_d[t][:], ALU.add)
+            nc.vector.tensor_tensor(m1[t][:].indirect(l_n1[:]), half_y[t], picked_d[t], ALU.add)
 
-        b = []
         for t in range(PACK):
             b_bank = bank(t)
             product(b_bank[:], w3_q, t, x_three)
-            b.append(leave_bank(f"b_{t}", b_bank))
+            nc.scalar.copy(b[t][:, :S], b_bank[:])
         w4_bf16 = cast_weight("w4", w4_raw)
 
         h_banks = [bank(PACK + t) for t in range(PACK)]
@@ -169,27 +169,29 @@ def tile_picked_trioputbpathbharm_none_p_kernel(
         z_bf16 = [keep.tile([P, PACK * PIECE], BF16, name=f"z_bf16_{piece}", align_bytes=64) for piece in range(S // PIECE)]
         w4_q = quantize("w4", w4_bf16)
 
-        def fetch_m1(piece, t):
-            entries = slice(piece * PIECE // STRIPE, (piece + 1) * PIECE // STRIPE)
-            first_m = ring.tile([P, PIECE], F32, name="first_m")
-            second_m = ring.tile([P, PIECE], F32, name="second_m")
+        def make_z(t, cols):
+            width = cols.stop - cols.start
+            entries = slice(cols.start // STRIPE, cols.stop // STRIPE)
+            first_m = keep.tile([P, width], F32, name="w3_bf16", align_bytes=64)
+            second_m = keep.tile([P, width], F32, name="second_m")
+            if t == LAST and cols.stop == S:
+                first = keep.tile([P, width], F32, name="z_bf16_0", align_bytes=64)
+            else:
+                first = ring.tile([P, width], F32, name="first")
+            second = ring.tile([P, width], F32, name="second")
             nc.vector.tensor_copy(first_m[:], m1[t][:].indirect(l_n3[:, entries]))
             nc.vector.tensor_copy(second_m[:], m1[t][:].indirect(l_n4[:, entries]))
-            return first_m, second_m
-
-        def add_b(piece, t, first_m, second_m):
-            entries = slice(piece * PIECE // STRIPE, (piece + 1) * PIECE // STRIPE)
-            first = ring.tile([P, PIECE], F32, name="first")
-            second = ring.tile([P, PIECE], F32, name="second")
             nc.vector.tensor_tensor(first[:], b[t][:].indirect(l_n5[:, entries]), first_m[:], ALU.add)
             nc.vector.tensor_tensor(second[:], b[t][:].indirect(l_n6[:, entries]), second_m[:], ALU.add)
-            return first, second
-
-        def make_z(piece, t, first, second):
-            larger = h_pairs[t][:, S + piece * PIECE : S + (piece + 1) * PIECE]
+            larger = h_pairs[t][:, S + cols.start : S + cols.stop]
             nc.vector.tensor_tensor(larger, first[:], second[:], ALU.max)
-            z_planes = z_bf16[piece][:].rearrange("p (j t) -> p j t", t=PACK)
-            nc.scalar.activation(z_planes[:, :, t], larger, ACT.Copy, scale=gain[t][:])
+            for piece in range(cols.start // PIECE, cols.stop // PIECE):
+                z_planes = z_bf16[piece][:].rearrange("p (j t) -> p j t", t=PACK)
+                lo = piece * PIECE - cols.start
+                if t == LAST and cols.stop == S:
+                    nc.vector.tensor_scalar(z_planes[:, :, t], larger[:, lo : lo + PIECE], gain[t][:], None, ALU.mult)
+                else:
+                    nc.scalar.activation(z_planes[:, :, t], larger[:, lo : lo + PIECE], ACT.Copy, scale=gain[t][:])
 
         def make_h(piece):
             cols = slice(piece * PIECE, (piece + 1) * PIECE)
@@ -197,48 +199,58 @@ def tile_picked_trioputbpathbharm_none_p_kernel(
             for t in range(PACK):
                 product(h_banks[t][:, cols], w4_q, t, z_q)
             for t in range(PACK):
-                nc.scalar.copy(h_pairs[t][:, cols], h_banks[t][:, cols])
+                if piece == 1 and t == 0:
+                    nc.vector.tensor_copy(h_pairs[t][:, cols], h_banks[t][:, cols])
+                else:
+                    nc.scalar.copy(h_pairs[t][:, cols], h_banks[t][:, cols])
             for t in range(PACK):
                 nc.scalar.activation(h_squares[t][:, cols], h_banks[t][:, cols], ACT.Square)
 
-        steps = [(piece, t) for piece in range(S // PIECE) for t in range(PACK)]
-        pending = None
-        for number, step in enumerate(steps):
-            fetched = fetch_m1(*step)
-            if pending is not None:
-                make_z(*steps[number - 1], *pending)
-            pending = add_b(*step, *fetched)
-            if step == (1, 0):
-                make_h(0)
-        make_z(*steps[-1], *pending)
-        make_h(1)
+        for t in range(LAST):
+            make_z(t, slice(0, S))
+        for piece in range(S // PIECE):
+            make_z(LAST, slice(piece * PIECE, (piece + 1) * PIECE))
+            make_h(piece)
 
         out_rows = out.rearrange("(u t i) j -> t u i j", t=PACK, i=PACK)
         partner = [keep.tile([P, S], F32, name=f"partner{t}") for t in range(PACK)]
         top = [keep.tile([P, S], F32, name=f"top{t}") for t in range(PACK)]
-        squares = [keep.tile([P, S], F32, name=f"square{t}") for t in range(PACK)]
         blocks = [slice(c, c + P) for c in range(0, S, P)]
-        turned = []
-        for t in range(PACK):
+
+        def sum_of_squares(t):
             nc.vector.tensor_copy(partner[t][:], h_pairs[t][:].indirect(l_n7[:]))
-            nc.scalar.activation(squares[t][:], partner[t][:], ACT.Square)
+            square = keep.tile([P, S], F32, name=f"scratch{t % LAST}")
+            nc.scalar.activation(square[:], partner[t][:], ACT.Square)
             both = bank(t)
             for block in blocks:
                 nc.tensor.matmul(both[:, block], h_squares[t][:, block], identity[:], start=True, stop=False, is_transpose=True)
-                nc.tensor.matmul(both[:, block], squares[t][:, block], identity[:], start=False, stop=True, is_transpose=True)
-            turned.append(both)
-        inverse = []
+                nc.tensor.matmul(both[:, block], square[:, block], identity[:], start=False, stop=True, is_transpose=True)
+            return both
+
+        def invert(t, both, parts):
+            root = keep.tile([P, S], F32, name=f"scratch{t % LAST}")
+            inverse_turned = keep.tile([P, S], F32, name=f"inverse_turned{t}")
+            backs = []
+            for number, cols in parts:
+                nc.scalar.activation(root[:, cols], both[:, cols], ACT.Abs_reciprocal_sqrt, bias=0.5)
+                nc.scalar.activation(inverse_turned[:, cols], root[:, cols], ACT.Square)
+                back = bank(number)
+                for c in range(cols.start, cols.stop, P):
+                    nc.tensor.transpose(back[:, c : c + P], inverse_turned[:, c : c + P], identity[:])
+                backs.append((back, cols))
+            return backs
+
+        whole = slice(0, S)
+        turned = [sum_of_squares(t) for t in range(LAST)]
+        inverse = [invert(0, turned[0], [(0, whole)])]
+        turned.append(sum_of_squares(LAST))
         for t in range(PACK):
-            root = ring.tile([P, S], F32, name="root")
-            inverse_turned = ring.tile([P, S], F32, name="inverse_turned")
             nc.vector.scalar_tensor_tensor(top[t][:], h_banks[t][:], 2.0, partner[t][:], ALU.mult, ALU.mult)
-            nc.scalar.activation(root[:], turned[t][:], ACT.Abs_reciprocal_sqrt, bias=0.5)
-            nc.scalar.activation(inverse_turned[:], root[:], ACT.Square)
-            back = bank(t)
-            for block in blocks:
-                nc.tensor.transpose(back[:, block], inverse_turned[:, block], identity[:])
-            inverse.append(back)
+        for t in range(1, LAST):
+            inverse.append(invert(t, turned[t], [(t, whole)]))
+        inverse.append(invert(LAST, turned[LAST], [(PACK, slice(0, PIECE)), (PACK + 1, slice(PIECE, S))]))
         for t in range(PACK):
-            result = ring.tile([P, S], F32, name="result")
-            nc.vector.tensor_tensor(result[:], inverse[t][:], top[t][:], ALU.mult)
-            nc.sync.dma_start(out_rows[t], result[:])
+            for back, cols in inverse[t]:
+                result = keep.tile([P, cols.stop - cols.start], F32, name=f"result{t}_{cols.start}")
+                nc.vector.tensor_tensor(result[:], back[:, cols], top[t][:, cols], ALU.mult)
+                nc.sync.dma_start(out_rows[t][:, :, cols], result[:])

@@ -74,21 +74,21 @@ def tile_picked_trioputbpathbharm_none_p_kernel(
             )
 
         scale_table = keep.tile([P, T], U8, name="scale_table", align_bytes=64)
+        nc.gpsimd.memset(scale_table[:].bitcast(I32), 0)
         identity = keep.tile([P, P], F32, name="identity")
         make_identity(nc, identity[:])
         l_offs = load_list("l_offs", offs)
-        for q in range(4):
-            rows = x_scales[0, 4 * q : 4 * q + 4, :].bitcast(I32)
-            nc.sync.dma_start(scale_table[32 * q : 32 * q + 32, :].bitcast(I32), rows.unsqueeze(0).broadcast_to([8, 4, T // 4]))
         warm = keep.tile([P, 2], F32, name="warm")
         nc.vector.memset(warm[:, 0:1], 1.0)
         nc.scalar.activation(warm[:, 1:2], warm[:, 0:1], ACT.Abs_reciprocal_sqrt)
 
         l_two = load_list("l_two", two)
+        l_three = load_list("l_three", three)
+        for q in range(4):
+            nc.sync.dma_start(scale_table[32 * q : 32 * q + 4, :].bitcast(I32), x_scales[0, 4 * q : 4 * q + 4, :].bitcast(I32))
+        w1_raw = load_weight("w1", w1, 1)
         word_table = keep.tile([P, T], I32, name="word_table", align_bytes=64)
         nc.sync.dma_start(word_table[:], x_words[0].rearrange("p n t -> p (n t)").bitcast(I32))
-        l_three = load_list("l_three", three)
-        w1_raw = load_weight("w1", w1, 2)
         w2_raw = load_weight("w2", w2, 2)
         l_n1 = load_list("l_n1", n1)
         l_n2 = load_list("l_n2", n2)
@@ -128,10 +128,10 @@ def tile_picked_trioputbpathbharm_none_p_kernel(
 
         s_offs = pick_scales("x_offs", l_offs)
         s_two = pick_scales("x_two", l_two)
+        s_three = pick_scales("x_three", l_three)
         w1_bf16 = cast_weight("w1", w1_raw)
         x_offs = (pick_words("x_offs_words", l_offs), s_offs)
         x_two = (pick_words("x_two_words", l_two), s_two)
-        s_three = pick_scales("x_three", l_three)
         w1_q = quantize("w1", w1_bf16)
         w2_bf16 = cast_weight("w2", w2_raw)
         y_banks = [bank(t) for t in range(PACK)]
@@ -174,11 +174,11 @@ def tile_picked_trioputbpathbharm_none_p_kernel(
             entries = slice(cols.start // STRIPE, cols.stop // STRIPE)
             first_m = keep.tile([P, width], F32, name="w3_bf16", align_bytes=64)
             second_m = keep.tile([P, width], F32, name="second_m")
+            first = ring.tile([P, width], F32, name="first")
             if t == LAST and cols.stop == S:
-                first = keep.tile([P, width], F32, name="z_bf16_0", align_bytes=64)
+                second = keep.tile([P, width], F32, name="z_bf16_0", align_bytes=64)
             else:
-                first = ring.tile([P, width], F32, name="first")
-            second = ring.tile([P, width], F32, name="second")
+                second = ring.tile([P, width], F32, name="second")
             nc.vector.tensor_copy(first_m[:], m1[t][:].indirect(l_n3[:, entries]))
             nc.vector.tensor_copy(second_m[:], m1[t][:].indirect(l_n4[:, entries]))
             nc.vector.tensor_tensor(first[:], b[t][:].indirect(l_n5[:, entries]), first_m[:], ALU.add)

from contextlib import ExitStack

import concourse.mybir as mybir
from concourse.masks import make_identity

K, T, S, N, H, W = 512, 2048, 512, 512, 512, 256
FLOPS = 4 * 2 * 512 * 512 * 512

F32 = mybir.dt.float32
BF16 = mybir.dt.bfloat16
I32 = mybir.dt.int32
U32 = mybir.dt.uint32
U16 = mybir.dt.uint16
U8 = mybir.dt.uint8
FP8X4 = mybir.dt.float8_e4m3fn_x4
ALU = mybir.AluOpType
ACT = mybir.ActivationFunctionType

P = 128
PACK = 4
STRIPE = 16
PIECE = 256


def tile_picked_trioputbpathbharm_none_p_kernel(
    tc, x_words, x_scales, w1, w2, w3, gn, w4, offs, two, three, n1, n2, n3, n4, n5, n6, n7, out
):
    nc = tc.nc
    with ExitStack() as ctx:
        keep = ctx.enter_context(tc.tile_pool(name="keep", bufs=1))
        ring = ctx.enter_context(tc.tile_pool(name="ring", bufs=3))
        psum = ctx.enter_context(tc.psum_pool(name="psum", bufs=1))

        def load_list(name, src):
            tile = keep.tile(list(src.shape), U16, name=name)
            nc.sync.dma_start(tile[:], src)
            return tile

        def load_weight(name, src, parts):
            width = H // parts
            view = src.rearrange("(p j) c -> p j c", j=PACK)
            raws = []
            for part in range(parts):
                raw = keep.tile([P, PACK, width], F32, name=f"{name}_raw{part}")
                nc.sync.dma_start(raw[:], view[:, :, part * width : (part + 1) * width])
                raws.append(raw)
            return raws

        def cast_weight(name, raws):
            grouped = keep.tile([P, PACK * H], BF16, name=f"{name}_bf16", align_bytes=64)
            dealt = grouped[:].rearrange("p (t u i j) -> p t u j i", t=PACK, i=PACK, j=PACK)
            groups = P // PACK // len(raws)
            for part, raw in enumerate(raws):
                nc.scalar.copy(dealt[:, :, part * groups : (part + 1) * groups], raw[:].rearrange("p j (u t i) -> p t u j i", t=PACK, i=PACK))
            return grouped

        def quantize(name, grouped):
            width = grouped.shape[1] // PACK
            codes = keep.tile([P, width], U32, name=f"{name}_codes", align_bytes=64)
            scales = keep.tile([P, width], U8, name=f"{name}_scales", align_bytes=64)
            nc.vector.quantize_mx(out=codes[:].bitcast(FP8X4), scales=scales[:], in_=grouped[:])
            return codes, scales

        def product(bank, weight, t, moving):
            cols = slice(t * P, (t + 1) * P)
            nc.tensor.matmul_mx(
                out=bank,
                lhsT=weight[0][:, cols].bitcast(FP8X4),
                lhsT_scale=weight[1][:, cols],
                rhs=moving[0][:].bitcast(FP8X4),
                rhs_scale=moving[1][:],
                start=True,
                stop=True,
            )

        scale_table = keep.tile([P, T], U8, name="scale_table", align_bytes=64)
        nc.gpsimd.memset(scale_table[:].bitcast(I32), 0)
        identity = keep.tile([P, P], F32, name="identity")
        make_identity(nc, identity[:])
        l_offs = load_list("l_offs", offs)
        warm = keep.tile([P, 2], F32, name="warm")
        nc.vector.memset(warm[:, 0:1], 1.0)
        nc.scalar.activation(warm[:, 1:2], warm[:, 0:1], ACT.Abs_reciprocal_sqrt)

        l_two = load_list("l_two", two)
        l_three = load_list("l_three", three)
        for q in range(4):
            nc.sync.dma_start(scale_table[32 * q : 32 * q + 4, :].bitcast(I32), x_scales[0, 4 * q : 4 * q + 4, :].bitcast(I32))
        w1_raw = load_weight("w1", w1, 1)
        word_table = keep.tile([P, T], I32, name="word_table", align_bytes=64)
        nc.sync.dma_start(word_table[:], x_words[0].rearrange("p n t -> p (n t)").bitcast(I32))
        w2_raw = load_weight("w2", w2, 2)
        l_n1 = load_list("l_n1", n1)
        l_n2 = load_list("l_n2", n2)
        w3_raw = load_weight("w3", w3, 1)
        l_n3 = load_list("l_n3", n3)
        l_n5 = load_list("l_n5", n5)
        l_n4 = load_list("l_n4", n4)
        l_n6 = load_list("l_n6", n6)
        gain = [keep.tile([P, 1], F32, name=f"gain{t}") for t in range(PACK)]
        for t in range(PACK):
            nc.sync.dma_start(gain[t][:], gn.rearrange("(u t i) o -> t u i o", t=PACK, i=PACK)[t])
        w4_tile = keep.tile([P, PACK, N], F32, name="w4_raw")
        for t in range(PACK):
            nc.sync.dma_start(w4_tile[:, t, :], w4.rearrange("(u t i) c -> t u i c", t=PACK, i=PACK)[t])
        w4_raw = [w4_tile]
        l_n7 = load_list("l_n7", n7)

        def pick_scales(name, lst):
            picked = keep.tile([P, S], U8, name=f"{name}_scales", align_bytes=64)
            nc.vector.tensor_copy(picked[:], scale_table[:].indirect(lst[:]))
            return picked

        def pick_words(name, lst):
            picked = keep.tile([P, S], U32, name=name, align_bytes=64)
            nc.vector.tensor_copy(picked[:], word_table[:].bitcast(U32).indirect(lst[:]))
            return picked

        def bank(number):
            return psum.tile([P, S], F32, name=f"bank{number}")

        LAST = PACK - 1
        m1 = [keep.tile([P, S if t == LAST else 2 * S], F32, name=f"m1_{t}") for t in range(PACK)]
        b = [keep.tile([P, 2 * S], F32, name=f"b_{t}") for t in range(PACK)]
        d = [keep.tile([P, S], F32, name=f"d_{t}") for t in range(PACK)]
        for t in range(LAST):
            nc.gpsimd.memset(m1[t][:, S:], 0.0)

        s_offs = pick_scales("x_offs", l_offs)
        s_two = pick_scales("x_two", l_two)
        s_three = pick_scales("x_three", l_three)
        w1_bf16 = cast_weight("w1", w1_raw)
        x_offs = (pick_words("x_offs_words", l_offs), s_offs)
        x_two = (pick_words("x_two_words", l_two), s_two)
        w1_q = quantize("w1", w1_bf16)
        w2_bf16 = cast_weight("w2", w2_raw)
        y_banks = [bank(t) for t in range(PACK)]
        for t in range(PACK):
            product(y_banks[t][:], w1_q, t, x_offs)
        x_three = (pick_words("w1_bf16", l_three), s_three)
        w2_q = quantize("w2", w2_bf16)
        d_banks = [bank(PACK + t) for t in range(PACK)]
        for t in range(PACK):
            product(d_banks[t][:], w2_q, t, x_two)

        for t in range(PACK):
            nc.scalar.copy(m1[t][:, :S], y_banks[t][:])
            nc.scalar.copy(d[t][:], d_banks[t][:])
        w3_bf16 = cast_weight("w3", w3_raw)

        half_y = [b[t][:, S : S + W] for t in range(PACK)]
        picked_d = [b[t][:, S + W :] for t in range(PACK)]
        for t in range(PACK):
            nc.vector.tensor_scalar(half_y[t], m1[t][:].indirect(l_n1[:]), -0.5, 0.0, ALU.mult, ALU.add)
            nc.vector.tensor_copy(picked_d[t], d[t][:].indirect(l_n2[:]))
        w3_q = quantize("w3", w3_bf16)
        for t in range(PACK):
            nc.vector.tensor_tensor(m1[t][:].indirect(l_n1[:]), half_y[t], picked_d[t], ALU.add)

        for t in range(PACK):
            b_bank = bank(t)
            product(b_bank[:], w3_q, t, x_three)
            nc.scalar.copy(b[t][:, :S], b_bank[:])
        w4_bf16 = cast_weight("w4", w4_raw)

        h_banks = [bank(PACK + t) for t in range(PACK)]
        h_pairs = [keep.tile([P, 2 * S], F32, name=f"h_pair{t}") for t in range(PACK)]
        h_squares = [keep.tile([P, S], F32, name=f"h_square{t}") for t in range(PACK)]
        z_bf16 = [keep.tile([P, PACK * PIECE], BF16, name=f"z_bf16_{piece}", align_bytes=64) for piece in range(S // PIECE)]
        w4_q = quantize("w4", w4_bf16)

        def make_z(t, cols):
            width = cols.stop - cols.start
            entries = slice(cols.start // STRIPE, cols.stop // STRIPE)
            first_m = keep.tile([P, width], F32, name="w3_bf16", align_bytes=64)
            second_m = keep.tile([P, width], F32, name="second_m")
            first = ring.tile([P, width], F32, name="first")
            if t == LAST and cols.stop == S:
                second = keep.tile([P, width], F32, name="z_bf16_0", align_bytes=64)
            else:
                second = ring.tile([P, width], F32, name="second")
            nc.vector.tensor_copy(first_m[:], m1[t][:].indirect(l_n3[:, entries]))
            nc.vector.tensor_copy(second_m[:], m1[t][:].indirect(l_n4[:, entries]))
            nc.vector.tensor_tensor(first[:], b[t][:].indirect(l_n5[:, entries]), first_m[:], ALU.add)
            nc.vector.tensor_tensor(second[:], b[t][:].indirect(l_n6[:, entries]), second_m[:], ALU.add)
            larger = h_pairs[t][:, S + cols.start : S + cols.stop]
            nc.vector.tensor_tensor(larger, first[:], second[:], ALU.max)
            for piece in range(cols.start // PIECE, cols.stop // PIECE):
                z_planes = z_bf16[piece][:].rearrange("p (j t) -> p j t", t=PACK)
                lo = piece * PIECE - cols.start
                if t == LAST and cols.stop == S:
                    nc.vector.tensor_scalar(z_planes[:, :, t], larger[:, lo : lo + PIECE], gain[t][:], None, ALU.mult)
                else:
                    nc.scalar.activation(z_planes[:, :, t], larger[:, lo : lo + PIECE], ACT.Copy, scale=gain[t][:])

        def make_h(piece):
            cols = slice(piece * PIECE, (piece + 1) * PIECE)
            z_q = quantize(f"z{piece}", z_bf16[piece])
            for t in range(PACK):
                product(h_banks[t][:, cols], w4_q, t, z_q)
            for t in range(PACK):
                if piece == 1 and t == 0:
                    nc.vector.tensor_copy(h_pairs[t][:, cols], h_banks[t][:, cols])
                else:
                    nc.scalar.copy(h_pairs[t][:, cols], h_banks[t][:, cols])
            for t in range(PACK):
                nc.scalar.activation(h_squares[t][:, cols], h_banks[t][:, cols], ACT.Square)

        for t in range(LAST):
            make_z(t, slice(0, S))
        for piece in range(S // PIECE):
            make_z(LAST, slice(piece * PIECE, (piece + 1) * PIECE))
            make_h(piece)

        out_rows = out.rearrange("(u t i) j -> t u i j", t=PACK, i=PACK)
        partner = [keep.tile([P, S], F32, name=f"partner{t}") for t in range(PACK)]
        top = [keep.tile([P, S], F32, name=f"top{t}") for t in range(PACK)]
        blocks = [slice(c, c + P) for c in range(0, S, P)]

        def sum_of_squares(t):
            nc.vector.tensor_copy(partner[t][:], h_pairs[t][:].indirect(l_n7[:]))
            square = keep.tile([P, S], F32, name=f"scratch{t % LAST}")
            nc.scalar.activation(square[:], partner[t][:], ACT.Square)
            both = bank(t)
            for block in blocks:
                nc.tensor.matmul(both[:, block], h_squares[t][:, block], identity[:], start=True, stop=False, is_transpose=True)
                nc.tensor.matmul(both[:, block], square[:, block], identity[:], start=False, stop=True, is_transpose=True)
            return both

        def invert(t, both, parts):
            root = keep.tile([P, S], F32, name=f"scratch{t % LAST}")
            inverse_turned = keep.tile([P, S], F32, name=f"inverse_turned{t}")
            backs = []
            for number, cols in parts:
                nc.scalar.activation(root[:, cols], both[:, cols], ACT.Abs_reciprocal_sqrt, bias=0.5)
                nc.scalar.activation(inverse_turned[:, cols], root[:, cols], ACT.Square)
                back = bank(number)
                for c in range(cols.start, cols.stop, P):
                    nc.tensor.transpose(back[:, c : c + P], inverse_turned[:, c : c + P], identity[:])
                backs.append((back, cols))
            return backs

        whole = slice(0, S)
        turned = [sum_of_squares(t) for t in range(LAST)]
        inverse = [invert(0, turned[0], [(0, whole)])]
        turned.append(sum_of_squares(LAST))
        for t in range(PACK):
            nc.vector.scalar_tensor_tensor(top[t][:], h_banks[t][:], 2.0, partner[t][:], ALU.mult, ALU.mult)
        for t in range(1, LAST):
            inverse.append(invert(t, turned[t], [(t, whole)]))
        inverse.append(invert(LAST, turned[LAST], [(PACK, slice(0, PIECE)), (PACK + 1, slice(PIECE, S))]))
        for t in range(PACK):
            for back, cols in inverse[t]:
                result = keep.tile([P, cols.stop - cols.start], F32, name=f"result{t}_{cols.start}")
                nc.vector.tensor_tensor(result[:], back[:, cols], top[t][:, cols], ALU.mult)
                nc.sync.dma_start(out_rows[t][:, :, cols], result[:])
